import numpy as np
import ml_dtypes


def mxq(x, axis, fmt="e4m3"):
    dtype, down = {"e4m3": (ml_dtypes.float8_e4m3fn, 7), "e5m2": (ml_dtypes.float8_e5m2, 14)}[fmt]
    v = np.moveaxis(np.asarray(x, np.float32).astype(ml_dtypes.bfloat16).astype(np.float64), axis, -1)
    blocks = v.reshape(v.shape[:-1] + (-1, 32))
    amax = np.abs(blocks).max(-1, keepdims=True)
    byte = np.maximum(np.where(amax > 0, np.frexp(amax)[1] - 1 + 127, 0) - down, 1)
    scale = np.exp2(byte - 127.0)
    codes = (blocks / scale).astype(np.float32).astype(dtype).astype(np.float64)
    return np.moveaxis((codes * scale).reshape(v.shape), -1, axis)


WIDE = False


def mx_kscale(k):
    if not WIDE:
        return np.ones(k)
    levels = np.array([10, -10, 5, -5, 0])
    if k % 512:
        return np.exp2(np.random.permutation(np.resize(levels, k // 32))).repeat(32)
    a = np.empty((k // 512, 16))
    for p in range(k // 512):
        a[p, :8] = np.random.permutation(np.resize(levels, 8))
        for g in range(8):
            far = levels[np.abs(levels - a[p, g]) >= 10]
            a[p, g + 8] = far[np.random.randint(len(far))]
    return np.exp2(a.ravel()).repeat(32)


def f64(x):
    return np.asarray(x).astype(np.float64)


def striped(idx):
    return np.tile(idx.reshape(-1, 16).T, (8, 1)).astype(np.uint16)


def unstriped(offs):
    return offs[:16].T.reshape(-1).astype(np.int64)


def pack_weight(w):
    k, n = w.shape
    w = f64(np.asarray(w, np.float32).astype(ml_dtypes.bfloat16)).reshape(k // 32, 32, n)
    amax = np.abs(w).max(1)
    byte = np.clip(np.where(amax > 0, np.frexp(amax)[1] - 1 + 127 - 7, 1), 1, 254)
    scaled = (w * np.exp2(127.0 - byte)[:, None, :]).reshape(k, n).astype(np.float32)
    words = np.ascontiguousarray(scaled.reshape(k // 512, 128, 4, n).transpose(0, 1, 3, 2)).astype(ml_dtypes.float8_e4m3fn).view(np.uint8)
    return words, np.ascontiguousarray(byte.astype(np.uint8).reshape(k // 512, 16, n))


def unpack_weight(words, scales):
    g, p, n, _ = words.shape
    vals = np.ascontiguousarray(words).view(ml_dtypes.float8_e4m3fn).astype(np.float64) * np.repeat(np.exp2(scales.astype(np.float64) - 127.0), 8, axis=1)[..., None]
    return vals.transpose(0, 1, 3, 2).reshape(g * 512, n)


E2M1 = np.array([0.0, 0.5, 1.0, 1.5, 2.0, 3.0, 4.0, 6.0, -0.0, -0.5, -1.0, -1.5, -2.0, -3.0, -4.0, -6.0])


def pack_fp4(w):
    k, n = w.shape
    w = f64(np.asarray(w, np.float32).astype(ml_dtypes.bfloat16)).reshape(k // 32, 32, n)
    amax = np.abs(w).max(1)
    mant, ex = np.frexp(amax / 6.0)
    byte = np.clip(np.where(amax > 0, np.where(mant > 0.5, ex, ex - 1) + 127, 1), 1, 254)
    scaled = (w * np.exp2(127.0 - byte)[:, None, :]).reshape(k, n).astype(np.float32)
    c = np.ascontiguousarray(scaled.reshape(k // 512, 128, 4, n).transpose(0, 1, 3, 2)).astype(ml_dtypes.float4_e2m1fn).view(np.uint8) & 0xF
    words = (c[..., 0::2] | (c[..., 1::2] << 4)).reshape(k // 512, 128, 2 * n)
    return np.ascontiguousarray(words), np.ascontiguousarray(byte.astype(np.uint8).reshape(k // 512, 16, n))


def unpack_fp4(words, scales):
    g, _, n = scales.shape
    words = np.ascontiguousarray(words).reshape(g, 128, n, 2)
    nib = np.empty((g, 128, n, 4), np.uint8)
    nib[..., 0::2] = words & 0xF
    nib[..., 1::2] = words >> 4
    vals = E2M1[nib] * np.repeat(np.exp2(scales.astype(np.float64) - 127.0), 8, axis=1)[..., None]
    return vals.transpose(0, 1, 3, 2).reshape(g * 512, n)


def silu(v):
    return v / (1.0 + np.exp(-np.maximum(v, -700.0)))


K, T, S, H, N = 1024, 1024, 512, 512, 256
P = 2 ** 7


def setup_inputs():
    n = np.random.standard_normal
    s = mx_kscale(K)[:, None]
    u = mx_kscale(H)
    packed_xT = pack_weight(n((K, T)) * s)
    packed_w2 = pack_fp4(n((H, N)) / np.sqrt(H) / u[:, None])
    return {
        "x_words": packed_xT[0],
        "x_scales": packed_xT[1],
        "gate": np.tile(np.random.uniform(0.2, 1.0, S), (P, 1)).astype(np.float32),
        "res": n((N, T)).astype(np.float32),
        "w1": (n((K, H)) / np.sqrt(K) / s).astype(np.float32),
        "w3": (n((K, H)) / np.sqrt(K) / s * u).astype(np.float32),
        "w2_words": packed_w2[0],
        "w2_scales": packed_w2[1],
        "offs": striped(np.random.permutation(T)[:S]),
    }


def reference(x_words, x_scales, gate, res, w1, w3, w2_words, w2_scales, offs):
    r = f64(res)[:, unstriped(offs)]
    xq = unpack_weight(x_words, x_scales)[:, unstriped(offs)]
    h = (silu(mxq(f64(w1), 0, "e4m3").T @ xq)) * ((mxq(f64(w3), 0, "e4m3").T @ xq))
    y = unpack_fp4(w2_words, w2_scales).T @ mxq(h, 0, "e4m3")
    out = f64(res).copy()
    out[:, unstriped(offs)] = r + y * f64(gate)[:1]
    return out

@@ -1,0 +1,231 @@
+from contextlib import ExitStack
+
+import concourse.mybir as mybir
+from concourse.masks import make_identity
+
+K, T, S, H, N = 1024, 1024, 512, 512, 256
+FLOPS = 2 * S * (2 * K * H + H * N)
+
+F32 = mybir.dt.float32
+BF16 = mybir.dt.bfloat16
+I32 = mybir.dt.int32
+U32 = mybir.dt.uint32
+U16 = mybir.dt.uint16
+U8 = mybir.dt.uint8
+FP8X4 = mybir.dt.float8_e4m3fn_x4
+FP4X4 = mybir.dt.float4_e2m1fn_x4
+MULT = mybir.AluOpType.mult
+ADD = mybir.AluOpType.add
+SILU = mybir.ActivationFunctionType.Silu
+COPY = mybir.ActivationFunctionType.Copy
+
+P = 128
+PACK = 4
+PASSES = K // (P * PACK)
+CHUNK = 128
+CHUNKS = S // CHUNK
+HALF = S // 2
+BLOCKS = N // P
+
+
+def tile_picked_modres_glusilu_p_kernel(
+    tc, x_words, x_scales, gate, res, w1, w3, w2_words, w2_scales, offs, out
+):
+    nc = tc.nc
+    with ExitStack() as ctx:
+        keep = ctx.enter_context(tc.tile_pool(name="keep", bufs=1))
+        psum = ctx.enter_context(tc.psum_pool(name="psum", bufs=1))
+
+        def sb(name, shape, dtype):
+            return keep.tile(shape, dtype, name=name, align_bytes=64)
+
+        offsets = keep.tile([P, S // 16], U16, name="offsets")
+        xs_win = sb("xs_win", [P, T], U8)
+        w2_plane = sb("w2_plane", [P, N], U8)
+        gate_rows = sb("gate_rows", [P, P], F32)
+        warm = sb("warm", [P, 2], F32)
+        ident = sb("ident", [P, P], F32)
+
+        nc.gpsimd.memset(xs_win[:].bitcast(I32), 0)
+        nc.vector.memset(warm[:, 0:1], 0.0)
+        nc.scalar.activation(out=warm[:, 1:2], in_=warm[:, 0:1], func=SILU)
+        nc.gpsimd.memset(w2_plane[:].bitcast(I32), 0)
+        nc.gpsimd.memset(gate_rows[:], 0.0)
+        make_identity(nc, ident[:])
+
+        def load_w(name, w, z, c0, c1):
+            raw = sb(name, [P, PACK, c1 - c0], F32)
+            rows = w[z * P * PACK : (z + 1) * P * PACK, c0:c1]
+            nc.sync.dma_start(out=raw[:], in_=rows.rearrange("(p j) c -> p j c", j=PACK))
+            return raw
+
+        def load_x(z):
+            win = sb("xw%d" % z, [P, T], U32)
+            nc.sync.dma_start(out=win[:].bitcast(I32), in_=x_words[z].rearrange("p c r -> p (c r)").bitcast(I32))
+            return win
+
+        def load_res(name, b):
+            tile = sb(name, [P, T], F32)
+            nc.sync.dma_start(out=tile[:], in_=res[b * P : (b + 1) * P, :])
+            return tile
+
+        nc.sync.dma_start(offsets[:], offs)
+        xw = [load_x(0)]
+        for q in range(4):
+            nc.sync.dma_start(
+                out=xs_win[32 * q : 32 * q + 4 * PASSES, :].bitcast(I32),
+                in_=x_scales[:, 4 * q : 4 * q + 4, :].bitcast(I32),
+            )
+        xw.append(load_x(1))
+        raw10 = load_w("raw10", w1, 0, 0, H)
+        raw11 = load_w("raw11", w1, 1, 0, H)
+        nc.sync.dma_start(out=gate_rows[0:CHUNKS, :], in_=gate[0:1, :].rearrange("o (c j) -> (o c) j", j=CHUNK))
+        raw30 = load_w("raw30", w3, 0, 0, H)
+        raw31a = load_w("raw31a", w3, 1, 0, H // 2)
+        raw31b = load_w("raw31b", w3, 1, H // 2, H)
+        res_src = [load_res("res_src0", 0)]
+        w2_codes = sb("w2_codes", [P, 2 * N], U8)
+        nc.sync.dma_start(out=w2_codes[:].bitcast(I32), in_=w2_words[0].bitcast(I32))
+        for q in range(4):
+            nc.sync.dma_start(
+                out=w2_plane[32 * q : 32 * q + 4, :].bitcast(I32),
+                in_=w2_scales[0, 4 * q : 4 * q + 4, :].bitcast(I32),
+            )
+        res_src.append(load_res("res_src1", 1))
+        res_dst = [load_res("res_dst%d" % b, b) for b in range(BLOCKS)]
+
+        def bank(i, name, shape):
+            return psum.tile(shape, F32, name=name, tag="bank%d" % i)
+
+        gate_ps = bank(7, "gate_ps", [P, P])
+        nc.tensor.transpose(gate_ps[:], gate_rows[:], ident[:])
+        gate_col = sb("gate_col", [P, CHUNKS], F32)
+        nc.scalar.copy(out=gate_col[:], in_=gate_ps[:, 0:CHUNKS])
+
+        def cast(engine, wb, raw, m_first, m0, m1):
+            src = raw[:].rearrange("p j (m t) -> p m j t", t=PACK)[:, m0 - m_first : m1 - m_first]
+            dst = wb[:].rearrange("p t m j -> p m j t")[:, m0:m1]
+            if engine == "v":
+                nc.vector.tensor_copy(out=dst, in_=src)
+            else:
+                nc.scalar.copy(out=dst, in_=src)
+
+        def quant(wb, codes, plane, t, m0, m1):
+            cols = slice(t * P + m0, t * P + m1)
+            nc.vector.quantize_mx(
+                out=codes[:, cols].bitcast(FP8X4),
+                scales=plane[:, cols],
+                in_=wb[:, t, m0:m1, :].rearrange("p m j -> p (m j)"),
+            )
+
+        def quant_all(wb, codes, plane):
+            nc.vector.quantize_mx(out=codes[:].bitcast(FP8X4), scales=plane[:], in_=wb[:].rearrange("p t m j -> p (t m j)"))
+
+        def w_tiles(name):
+            return (sb(name + "_bf", [P, PACK, P, PACK], BF16), sb(name + "_codes", [P, H], U32), sb(name + "_plane", [P, H], U8))
+
+        q1 = [w_tiles("w1_%d" % z) for z in range(PASSES)]
+        q3 = [w_tiles("w3_%d" % z) for z in range(PASSES)]
+
+        xs_g = sb("xs_g", [P, S], U8)
+        xg = [sb("xg%d" % z, [P, S], U32) for z in range(PASSES)]
+
+        nc.vector.tensor_copy(xg[0][:], xw[0][:].indirect(offsets[:]))
+        nc.vector.tensor_copy(xs_g[:], xs_win[:].indirect(offsets[:]))
+        nc.vector.tensor_copy(xg[1][:], xw[1][:].indirect(offsets[:]))
+        cast("s", q1[0][0], raw10, 0, 0, 96)
+        cast("v", q1[0][0], raw10, 0, 96, P)
+        quant_all(*q1[0])
+        cast("v", q1[1][0], raw11, 0, 0, 80)
+        cast("s", q1[1][0], raw11, 0, 80, P)
+        quant_all(*q1[1])
+
+        def first_product(acc, qw, c):
+            cols = slice(c * CHUNK, (c + 1) * CHUNK)
+            for t in range(PACK):
+                for z in range(PASSES):
+                    nc.tensor.matmul_mx(
+                        out=acc[:, t, :],
+                        lhsT=qw[z][1][:, t * P : (t + 1) * P].bitcast(FP8X4),
+                        lhsT_scale=qw[z][2][:, t * P : (t + 1) * P],
+                        rhs=xg[z][:, cols].bitcast(FP8X4),
+                        rhs_scale=xs_g[4 * z : P, cols],
+                        start=(z == 0),
+                        stop=(z == PASSES - 1),
+                    )
+
+        act = []
+        for c in range(CHUNKS):
+            acc = bank(c, "acc1_%d" % c, [P, PACK, CHUNK])
+            first_product(acc, q1, c)
+            a = sb("act%d" % c, [P, CHUNK, PACK], F32)
+            nc.scalar.activation(out=a[:], in_=acc[:].rearrange("p t n -> p n t"), func=SILU)
+            act.append(a)
+
+        cast("v", q3[0][0], raw30, 0, 0, P)
+        quant_all(*q3[0])
+        cast("v", q3[1][0], raw31a, 0, 0, 64)
+        for t in range(PACK):
+            quant(*q3[1], t, 0, 64)
+        cast("v", q3[1][0], raw31b, 64, 64, 104)
+        cast("s", q3[1][0], raw31b, 64, 104, P)
+        for t in range(PACK):
+            quant(*q3[1], t, 64, P)
+
+        up = []
+        for c in range(CHUNKS):
+            acc = bank(CHUNKS + c, "acc3_%d" % c, [P, PACK, CHUNK])
+            first_product(acc, q3, c)
+            up.append(acc)
+
+        picked = [[sb("picked%d_%d" % (b, h), [P, HALF], F32) for h in range(2)] for b in range(BLOCKS)]
+        gated = [sb("gated%d" % h, [P, BLOCKS, HALF], F32) for h in range(2)]
+        hb = [sb("hb%d" % c, [P, CHUNK, PACK], BF16) for c in range(CHUNKS)]
+
+        def half_list(h):
+            return offsets[:, h * HALF // 16 : (h + 1) * HALF // 16]
+
+        def pick(b, h):
+            nc.vector.tensor_copy(picked[b][h][:], res_src[b][:].indirect(half_list(h)))
+
+        def hidden(c):
+            nc.vector.tensor_tensor(out=hb[c][:], in0=up[c][:].rearrange("p t n -> p n t"), in1=act[c][:], op=MULT)
+
+        def second(c):
+            codes = sb("h_codes%d" % c, [P, CHUNK], U32)
+            plane = sb("h_plane%d" % c, [P, CHUNK], U8)
+            nc.vector.quantize_mx(out=codes[:].bitcast(FP8X4), scales=plane[:], in_=hb[c][:].rearrange("p n t -> p (n t)"))
+            y_t = bank(c, "y_t%d" % c, [P, N])
+            nc.tensor.matmul_mx(
+                out=y_t[:], lhsT=codes[:].bitcast(FP8X4), lhsT_scale=plane[:],
+                rhs=w2_codes[:].bitcast(FP4X4), rhs_scale=w2_plane[:], start=True, stop=True,
+            )
+            g_t = sb("g_t%d" % c, [P, N], F32)
+            nc.scalar.activation(out=g_t[:], in_=y_t[:], func=COPY, scale=gate_col[:, c : c + 1])
+            y_n = bank(CHUNKS + c, "y_n%d" % c, [P, BLOCKS, CHUNK])
+            for b in range(BLOCKS):
+                nc.tensor.transpose(y_n[:, b, :], g_t[:, b * P : (b + 1) * P], ident[:])
+            h, j0 = divmod(c * CHUNK, HALF)
+            nc.scalar.copy(out=gated[h][:, :, j0 : j0 + CHUNK], in_=y_n[:])
+
+        def put(b, h):
+            nc.vector.tensor_tensor(res_dst[b][:].indirect(half_list(h)), gated[h][:, b, :], picked[b][h][:], ADD)
+
+        pick(0, 0)
+        hidden(0)
+        hidden(1)
+        second(0)
+        hidden(2)
+        second(1)
+        hidden(3)
+        second(2)
+        pick(1, 0)
+        second(3)
+        pick(0, 1)
+        pick(1, 1)
+        put(0, 0)
+        put(1, 0)
+        put(0, 1)
+        nc.sync.dma_start(out=out[0:P, :], in_=res_dst[0][:])
+        put(1, 1)
+        nc.sync.dma_start(out=out[P : 2 * P, :], in_=res_dst[1][:])

@@ -36,8 +36,8 @@ def tile_picked_modres_glusilu_p_kernel(
         keep = ctx.enter_context(tc.tile_pool(name="keep", bufs=1))
         psum = ctx.enter_context(tc.psum_pool(name="psum", bufs=1))
 
-        def sb(name, shape, dtype):
-            return keep.tile(shape, dtype, name=name, align_bytes=64)
+        def sb(name, shape, dtype, tag=None):
+            return keep.tile(shape, dtype, name=name, tag=tag or name, align_bytes=64)
 
         offsets = keep.tile([P, S // 16], U16, name="offsets")
         xs_win = sb("xs_win", [P, T], U8)
@@ -76,14 +76,14 @@ def tile_picked_modres_glusilu_p_kernel(
                 out=xs_win[32 * q : 32 * q + 4 * PASSES, :].bitcast(I32),
                 in_=x_scales[:, 4 * q : 4 * q + 4, :].bitcast(I32),
             )
-        xw.append(load_x(1))
         raw10 = load_w("raw10", w1, 0, 0, H)
         raw11 = load_w("raw11", w1, 1, 0, H)
+        xw.append(load_x(1))
         nc.sync.dma_start(out=gate_rows[0:CHUNKS, :], in_=gate[0:1, :].rearrange("o (c j) -> (o c) j", j=CHUNK))
         raw30 = load_w("raw30", w3, 0, 0, H)
         raw31a = load_w("raw31a", w3, 1, 0, H // 2)
         raw31b = load_w("raw31b", w3, 1, H // 2, H)
-        res_src = [load_res("res_src0", 0)]
+        res_src = [load_res("res_src%d" % b, b) for b in range(BLOCKS)]
         w2_codes = sb("w2_codes", [P, 2 * N], U8)
         nc.sync.dma_start(out=w2_codes[:].bitcast(I32), in_=w2_words[0].bitcast(I32))
         for q in range(4):
@@ -91,7 +91,6 @@ def tile_picked_modres_glusilu_p_kernel(
                 out=w2_plane[32 * q : 32 * q + 4, :].bitcast(I32),
                 in_=w2_scales[0, 4 * q : 4 * q + 4, :].bitcast(I32),
             )
-        res_src.append(load_res("res_src1", 1))
         res_dst = [load_res("res_dst%d" % b, b) for b in range(BLOCKS)]
 
         def bank(i, name, shape):
@@ -132,13 +131,17 @@ def tile_picked_modres_glusilu_p_kernel(
 
         nc.vector.tensor_copy(xg[0][:], xw[0][:].indirect(offsets[:]))
         nc.vector.tensor_copy(xs_g[:], xs_win[:].indirect(offsets[:]))
-        nc.vector.tensor_copy(xg[1][:], xw[1][:].indirect(offsets[:]))
-        cast("s", q1[0][0], raw10, 0, 0, 96)
-        cast("v", q1[0][0], raw10, 0, 96, P)
+        cast("s", q1[0][0], raw10, 0, 0, 64)
+        cast("v", q1[0][0], raw10, 0, 64, P)
         quant_all(*q1[0])
         cast("v", q1[1][0], raw11, 0, 0, 80)
         cast("s", q1[1][0], raw11, 0, 80, P)
         quant_all(*q1[1])
+        for c in range(CHUNKS):
+            nc.vector.tensor_copy(
+                xg[1][:, c * CHUNK : (c + 1) * CHUNK],
+                xw[1][:].indirect(offsets[:, c * CHUNK // 16 : (c + 1) * CHUNK // 16]),
+            )
 
         def first_product(acc, qw, c):
             cols = slice(c * CHUNK, (c + 1) * CHUNK)
@@ -154,23 +157,25 @@ def tile_picked_modres_glusilu_p_kernel(
                         stop=(z == PASSES - 1),
                     )
 
+        cast("v", q3[0][0], raw30, 0, 0, 80)
+        cast("s", q3[0][0], raw30, 0, 80, P)
+        quant_all(*q3[0])
+        cast("v", q3[1][0], raw31a, 0, 0, 32)
+        cast("s", q3[1][0], raw31a, 0, 32, 64)
+        for t in range(PACK):
+            quant(*q3[1], t, 0, 64)
+        cast("v", q3[1][0], raw31b, 64, 64, P)
+        for t in range(PACK):
+            quant(*q3[1], t, 64, P)
+
         act = []
+        act_all = sb("act_all", [P, CHUNKS, CHUNK, PACK], F32, tag="raw31a")
         for c in range(CHUNKS):
             acc = bank(c, "acc1_%d" % c, [P, PACK, CHUNK])
             first_product(acc, q1, c)
-            a = sb("act%d" % c, [P, CHUNK, PACK], F32)
-            nc.scalar.activation(out=a[:], in_=acc[:].rearrange("p t n -> p n t"), func=SILU)
+            a = act_all[:, c]
+            nc.scalar.activation(out=a, in_=acc[:].rearrange("p t n -> p n t"), func=SILU)
             act.append(a)
-
-        cast("v", q3[0][0], raw30, 0, 0, P)
-        quant_all(*q3[0])
-        cast("v", q3[1][0], raw31a, 0, 0, 64)
-        for t in range(PACK):
-            quant(*q3[1], t, 0, 64)
-        cast("v", q3[1][0], raw31b, 64, 64, 104)
-        cast("s", q3[1][0], raw31b, 64, 104, P)
-        for t in range(PACK):
-            quant(*q3[1], t, 64, P)
 
         up = []
         for c in range(CHUNKS):
@@ -178,24 +183,25 @@ def tile_picked_modres_glusilu_p_kernel(
             first_product(acc, q3, c)
             up.append(acc)
 
-        picked = [[sb("picked%d_%d" % (b, h), [P, HALF], F32) for h in range(2)] for b in range(BLOCKS)]
+        picked = {}
         gated = [sb("gated%d" % h, [P, BLOCKS, HALF], F32) for h in range(2)]
         hb = [sb("hb%d" % c, [P, CHUNK, PACK], BF16) for c in range(CHUNKS)]
 
         def half_list(h):
             return offsets[:, h * HALF // 16 : (h + 1) * HALF // 16]
 
-        def pick(b, h):
-            nc.vector.tensor_copy(picked[b][h][:], res_src[b][:].indirect(half_list(h)))
+        def pick(b, after):
+            picked[b] = sb("picked%d" % b, [P, S], F32, tag=after)
+            nc.vector.tensor_copy(picked[b][:], res_src[b][:].indirect(offsets[:]))
 
         def hidden(c):
-            nc.vector.tensor_tensor(out=hb[c][:], in0=up[c][:].rearrange("p t n -> p n t"), in1=act[c][:], op=MULT)
+            nc.vector.tensor_tensor(out=hb[c][:], in0=up[c][:].rearrange("p t n -> p n t"), in1=act[c], op=MULT)
 
         def second(c):
             codes = sb("h_codes%d" % c, [P, CHUNK], U32)
             plane = sb("h_plane%d" % c, [P, CHUNK], U8)
             nc.vector.quantize_mx(out=codes[:].bitcast(FP8X4), scales=plane[:], in_=hb[c][:].rearrange("p n t -> p (n t)"))
-            y_t = bank(c, "y_t%d" % c, [P, N])
+            y_t = bank(c if c < 2 else CHUNKS + c - 2, "y_t%d" % c, [P, N])
             nc.tensor.matmul_mx(
                 out=y_t[:], lhsT=codes[:].bitcast(FP8X4), lhsT_scale=plane[:],
                 rhs=w2_codes[:].bitcast(FP4X4), rhs_scale=w2_plane[:], start=True, stop=True,
@@ -209,9 +215,9 @@ def tile_picked_modres_glusilu_p_kernel(
             nc.scalar.copy(out=gated[h][:, :, j0 : j0 + CHUNK], in_=y_n[:])
 
         def put(b, h):
-            nc.vector.tensor_tensor(res_dst[b][:].indirect(half_list(h)), gated[h][:, b, :], picked[b][h][:], ADD)
+            nc.vector.tensor_tensor(res_dst[b][:].indirect(half_list(h)), gated[h][:, b, :], picked[b][:, h * HALF : (h + 1) * HALF], ADD)
 
-        pick(0, 0)
+        pick(0, "w3_1_bf")
         hidden(0)
         hidden(1)
         second(0)
@@ -219,10 +225,8 @@ def tile_picked_modres_glusilu_p_kernel(
         second(1)
         hidden(3)
         second(2)
-        pick(1, 0)
         second(3)
-        pick(0, 1)
-        pick(1, 1)
+        pick(1, "hb3")
         put(0, 0)
         put(1, 0)
         put(0, 1)

@@ -101,9 +101,9 @@ def tile_picked_modres_glusilu_p_kernel(
         gate_col = sb("gate_col", [P, CHUNKS], F32)
         nc.scalar.copy(out=gate_col[:], in_=gate_ps[:, 0:CHUNKS])
 
-        def cast(engine, wb, raw, m_first, m0, m1):
-            src = raw[:].rearrange("p j (m t) -> p m j t", t=PACK)[:, m0 - m_first : m1 - m_first]
-            dst = wb[:].rearrange("p t m j -> p m j t")[:, m0:m1]
+        def cast(engine, wb, raw, m_first, m0, m1, t0):
+            src = raw[:].rearrange("p j (m t) -> p m j t", t=PACK)[:, m0 - m_first : m1 - m_first, :, t0 : t0 + 2]
+            dst = wb[:].rearrange("p t m j -> p m j t")[:, m0:m1, :, t0 : t0 + 2]
             if engine == "v":
                 nc.vector.tensor_copy(out=dst, in_=src)
             else:
@@ -131,11 +131,12 @@ def tile_picked_modres_glusilu_p_kernel(
 
         nc.vector.tensor_copy(xg[0][:], xw[0][:].indirect(offsets[:]))
         nc.vector.tensor_copy(xs_g[:], xs_win[:].indirect(offsets[:]))
-        cast("s", q1[0][0], raw10, 0, 0, 64)
-        cast("v", q1[0][0], raw10, 0, 64, P)
+        cast("s", q1[0][0], raw10, 0, 0, P, 2)
+        cast("v", q1[0][0], raw10, 0, 0, P, 0)
         quant_all(*q1[0])
-        cast("v", q1[1][0], raw11, 0, 0, 80)
-        cast("s", q1[1][0], raw11, 0, 80, P)
+        cast("s", q1[1][0], raw11, 0, 32, P, 2)
+        cast("v", q1[1][0], raw11, 0, 0, P, 0)
+        cast("v", q1[1][0], raw11, 0, 0, 32, 2)
         quant_all(*q1[1])
         for c in range(CHUNKS):
             nc.vector.tensor_copy(
@@ -157,23 +158,23 @@ def tile_picked_modres_glusilu_p_kernel(
                         stop=(z == PASSES - 1),
                     )
 
-        cast("v", q3[0][0], raw30, 0, 0, 80)
-        cast("s", q3[0][0], raw30, 0, 80, P)
+        cast("s", q3[0][0], raw30, 0, 32, P, 2)
+        cast("v", q3[0][0], raw30, 0, 0, P, 0)
+        cast("v", q3[0][0], raw30, 0, 0, 32, 2)
         quant_all(*q3[0])
-        cast("v", q3[1][0], raw31a, 0, 0, 32)
-        cast("s", q3[1][0], raw31a, 0, 32, 64)
+        cast("s", q3[1][0], raw31a, 0, 0, 64, 2)
+        cast("v", q3[1][0], raw31a, 0, 0, 64, 0)
+        cast("s", q3[1][0], raw31b, 64, 64, P, 2)
+        cast("v", q3[1][0], raw31b, 64, 64, P, 0)
         for t in range(PACK):
-            quant(*q3[1], t, 0, 64)
-        cast("v", q3[1][0], raw31b, 64, 64, P)
-        for t in range(PACK):
-            quant(*q3[1], t, 64, P)
+            quant(*q3[1], t, 0, P)
 
         act = []
-        act_all = sb("act_all", [P, CHUNKS, CHUNK, PACK], F32, tag="raw31a")
+        late = sb("late", [P, (PACK + 1) * S], F32, tag="raw31b")
         for c in range(CHUNKS):
             acc = bank(c, "acc1_%d" % c, [P, PACK, CHUNK])
             first_product(acc, q1, c)
-            a = act_all[:, c]
+            a = late[:, c * CHUNK * PACK : (c + 1) * CHUNK * PACK].rearrange("p (n t) -> p n t", t=PACK)
             nc.scalar.activation(out=a, in_=acc[:].rearrange("p t n -> p n t"), func=SILU)
             act.append(a)
 
@@ -190,9 +191,9 @@ def tile_picked_modres_glusilu_p_kernel(
         def half_list(h):
             return offsets[:, h * HALF // 16 : (h + 1) * HALF // 16]
 
-        def pick(b, after):
-            picked[b] = sb("picked%d" % b, [P, S], F32, tag=after)
-            nc.vector.tensor_copy(picked[b][:], res_src[b][:].indirect(offsets[:]))
+        def pick(b, dst):
+            picked[b] = dst
+            nc.vector.tensor_copy(dst, res_src[b][:].indirect(offsets[:]))
 
         def hidden(c):
             nc.vector.tensor_tensor(out=hb[c][:], in0=up[c][:].rearrange("p t n -> p n t"), in1=act[c], op=MULT)
@@ -217,7 +218,7 @@ def tile_picked_modres_glusilu_p_kernel(
         def put(b, h):
             nc.vector.tensor_tensor(res_dst[b][:].indirect(half_list(h)), gated[h][:, b, :], picked[b][:, h * HALF : (h + 1) * HALF], ADD)
 
-        pick(0, "w3_1_bf")
+        pick(0, late[:, PACK * S :])
         hidden(0)
         hidden(1)
         second(0)
@@ -226,7 +227,7 @@ def tile_picked_modres_glusilu_p_kernel(
         hidden(3)
         second(2)
         second(3)
-        pick(1, "hb3")
+        pick(1, sb("picked1", [P, S], F32, tag="hb3")[:])
         put(0, 0)
         put(1, 0)
         put(0, 1)

@@ -43,12 +43,9 @@ def tile_picked_modres_glusilu_p_kernel(
         xs_win = sb("xs_win", [P, T], U8)
         w2_plane = sb("w2_plane", [P, N], U8)
         gate_rows = sb("gate_rows", [P, P], F32)
-        warm = sb("warm", [P, 2], F32)
         ident = sb("ident", [P, P], F32)
 
         nc.gpsimd.memset(xs_win[:].bitcast(I32), 0)
-        nc.vector.memset(warm[:, 0:1], 0.0)
-        nc.scalar.activation(out=warm[:, 1:2], in_=warm[:, 0:1], func=SILU)
         nc.gpsimd.memset(w2_plane[:].bitcast(I32), 0)
         nc.gpsimd.memset(gate_rows[:], 0.0)
         make_identity(nc, ident[:])

@@ -49,6 +49,9 @@ def tile_picked_modres_glusilu_p_kernel(
         nc.gpsimd.memset(w2_plane[:].bitcast(I32), 0)
         nc.gpsimd.memset(gate_rows[:], 0.0)
         make_identity(nc, ident[:])
+        warm = sb("warm", [P, 16], F32)
+        nc.gpsimd.memset(warm[:], 0.0)
+        nc.scalar.activation(out=warm[:, 8:9], in_=warm[:, 0:1], func=SILU)
 
         def load_w(name, w, z, c0, c1):
             raw = sb(name, [P, PACK, c1 - c0], F32)
@@ -106,6 +109,14 @@ def tile_picked_modres_glusilu_p_kernel(
             else:
                 nc.scalar.copy(out=dst, in_=src)
 
+        def cast_all(engine, wb, raw, m0, m1):
+            src = raw[:].rearrange("p j (m t) -> p m j t", t=PACK)[:, m0:m1]
+            dst = wb[:].rearrange("p t m j -> p m j t")[:, m0:m1]
+            if engine == "v":
+                nc.vector.tensor_copy(out=dst, in_=src)
+            else:
+                nc.scalar.copy(out=dst, in_=src)
+
         def quant(wb, codes, plane, t, m0, m1):
             cols = slice(t * P + m0, t * P + m1)
             nc.vector.quantize_mx(
@@ -128,12 +139,11 @@ def tile_picked_modres_glusilu_p_kernel(
 
         nc.vector.tensor_copy(xg[0][:], xw[0][:].indirect(offsets[:]))
         nc.vector.tensor_copy(xs_g[:], xs_win[:].indirect(offsets[:]))
-        cast("s", q1[0][0], raw10, 0, 0, P, 2)
-        cast("v", q1[0][0], raw10, 0, 0, P, 0)
+        cast_all("s", q1[0][0], raw10, 64, P)
+        cast_all("v", q1[0][0], raw10, 0, 64)
         quant_all(*q1[0])
-        cast("s", q1[1][0], raw11, 0, 32, P, 2)
-        cast("v", q1[1][0], raw11, 0, 0, P, 0)
-        cast("v", q1[1][0], raw11, 0, 0, 32, 2)
+        cast_all("s", q1[1][0], raw11, 72, P)
+        cast_all("v", q1[1][0], raw11, 0, 72)
         quant_all(*q1[1])
         for c in range(CHUNKS):
             nc.vector.tensor_copy(
@@ -155,9 +165,8 @@ def tile_picked_modres_glusilu_p_kernel(
                         stop=(z == PASSES - 1),
                     )
 
-        cast("s", q3[0][0], raw30, 0, 32, P, 2)
-        cast("v", q3[0][0], raw30, 0, 0, P, 0)
-        cast("v", q3[0][0], raw30, 0, 0, 32, 2)
+        cast_all("s", q3[0][0], raw30, 72, P)
+        cast_all("v", q3[0][0], raw30, 0, 72)
         quant_all(*q3[0])
         cast("s", q3[1][0], raw31a, 0, 0, 64, 2)
         cast("v", q3[1][0], raw31a, 0, 0, 64, 0)
@@ -167,7 +176,7 @@ def tile_picked_modres_glusilu_p_kernel(
             quant(*q3[1], t, 0, P)
 
         act = []
-        late = sb("late", [P, (PACK + 1) * S], F32, tag="raw31b")
+        late = sb("late", [P, PACK * S + HALF], F32, tag="raw31b")
         for c in range(CHUNKS):
             acc = bank(c, "acc1_%d" % c, [P, PACK, CHUNK])
             first_product(acc, q1, c)
@@ -183,25 +192,28 @@ def tile_picked_modres_glusilu_p_kernel(
 
         picked = {}
         gated = [sb("gated%d" % h, [P, BLOCKS, HALF], F32) for h in range(2)]
-        hb = [sb("hb%d" % c, [P, CHUNK, PACK], BF16) for c in range(CHUNKS)]
+        hb_last = sb("hb_last", [P, 2, CHUNK, PACK], BF16)
+        hb = [sb("hb0", [P, CHUNK, PACK], BF16)[:], sb("hb1", [P, CHUNK, PACK], BF16)[:], hb_last[:, 0], hb_last[:, 1]]
 
         def half_list(h):
             return offsets[:, h * HALF // 16 : (h + 1) * HALF // 16]
 
-        def pick(b, dst):
-            picked[b] = dst
-            nc.vector.tensor_copy(dst, res_src[b][:].indirect(offsets[:]))
+        def pick(b, dst, places):
+            nc.vector.tensor_copy(dst, res_src[b][:].indirect(places))
 
         def hidden(c):
-            nc.vector.tensor_tensor(out=hb[c][:], in0=up[c][:].rearrange("p t n -> p n t"), in1=act[c], op=MULT)
+            nc.vector.tensor_tensor(out=hb[c], in0=up[c][:].rearrange("p t n -> p n t"), in1=act[c], op=MULT)
 
-        def second(c):
-            codes = sb("h_codes%d" % c, [P, CHUNK], U32)
-            plane = sb("h_plane%d" % c, [P, CHUNK], U8)
-            nc.vector.quantize_mx(out=codes[:].bitcast(FP8X4), scales=plane[:], in_=hb[c][:].rearrange("p n t -> p (n t)"))
+        def quant_h(name, values, width, tag=None):
+            codes = sb("h_codes" + name, [P, width], U32, tag=tag)
+            plane = sb("h_plane" + name, [P, width], U8)
+            nc.vector.quantize_mx(out=codes[:].bitcast(FP8X4), scales=plane[:], in_=values)
+            return codes, plane
+
+        def second(c, codes, plane):
             y_t = bank(c if c < 2 else CHUNKS + c - 2, "y_t%d" % c, [P, N])
             nc.tensor.matmul_mx(
-                out=y_t[:], lhsT=codes[:].bitcast(FP8X4), lhsT_scale=plane[:],
+                out=y_t[:], lhsT=codes.bitcast(FP8X4), lhsT_scale=plane,
                 rhs=w2_codes[:].bitcast(FP4X4), rhs_scale=w2_plane[:], start=True, stop=True,
             )
             g_t = sb("g_t%d" % c, [P, N], F32)
@@ -213,18 +225,28 @@ def tile_picked_modres_glusilu_p_kernel(
             nc.scalar.copy(out=gated[h][:, :, j0 : j0 + CHUNK], in_=y_n[:])
 
         def put(b, h):
-            nc.vector.tensor_tensor(res_dst[b][:].indirect(half_list(h)), gated[h][:, b, :], picked[b][:, h * HALF : (h + 1) * HALF], ADD)
+            nc.vector.tensor_tensor(res_dst[b][:].indirect(half_list(h)), gated[h][:, b, :], picked[b, h], ADD)
 
-        pick(0, late[:, PACK * S :])
+        picked[0, 0] = late[:, PACK * S :]
+        pick(0, picked[0, 0], half_list(0))
         hidden(0)
         hidden(1)
-        second(0)
+        up_last = sb("up_last", [P, CHUNK, PACK], F32)
+        nc.scalar.copy(out=up_last[:], in_=up[3][:].rearrange("p t n -> p n t"))
+        nc.gpsimd.tensor_tensor(out=hb[3], in0=up_last[:], in1=act[3], op=MULT)
+        for c in range(2):
+            codes, plane = quant_h(str(c), hb[c].rearrange("p n t -> p (n t)"), CHUNK)
+            second(c, codes[:], plane[:])
+        block1 = sb("picked1", [P, S], F32, tag="h_codes0")
+        pick(1, block1[:], offsets[:])
+        picked[1, 0], picked[1, 1] = block1[:, 0:HALF], block1[:, HALF:S]
         hidden(2)
-        second(1)
-        hidden(3)
-        second(2)
-        second(3)
-        pick(1, sb("picked1", [P, S], F32, tag="hb3")[:])
+        picked[0, 1] = sb("picked01", [P, HALF], F32, tag="h_codes1")[:]
+        pick(0, picked[0, 1], half_list(1))
+        codes, plane = quant_h("23", hb_last[:].rearrange("p c n t -> p (c n t)"), 2 * CHUNK, tag="res_src1")
+        for c in (2, 3):
+            cols = slice((c - 2) * CHUNK, (c - 1) * CHUNK)
+            second(c, codes[:, cols], plane[:, cols])
         put(0, 0)
         put(1, 0)
         put(0, 1)

@@ -77,8 +77,8 @@ def tile_picked_modres_glusilu_p_kernel(
                 in_=x_scales[:, 4 * q : 4 * q + 4, :].bitcast(I32),
             )
         raw10 = load_w("raw10", w1, 0, 0, H)
-        raw11 = load_w("raw11", w1, 1, 0, H)
         xw.append(load_x(1))
+        raw11 = load_w("raw11", w1, 1, 0, H)
         nc.sync.dma_start(out=gate_rows[0:CHUNKS, :], in_=gate[0:1, :].rearrange("o (c j) -> (o c) j", j=CHUNK))
         raw30 = load_w("raw30", w3, 0, 0, H)
         raw31a = load_w("raw31a", w3, 1, 0, H // 2)
@@ -139,17 +139,13 @@ def tile_picked_modres_glusilu_p_kernel(
 
         nc.vector.tensor_copy(xg[0][:], xw[0][:].indirect(offsets[:]))
         nc.vector.tensor_copy(xs_g[:], xs_win[:].indirect(offsets[:]))
-        cast_all("s", q1[0][0], raw10, 64, P)
-        cast_all("v", q1[0][0], raw10, 0, 64)
+        cast_all("s", q1[0][0], raw10, 80, P)
+        cast_all("v", q1[0][0], raw10, 0, 80)
         quant_all(*q1[0])
-        cast_all("s", q1[1][0], raw11, 72, P)
-        cast_all("v", q1[1][0], raw11, 0, 72)
+        nc.vector.tensor_copy(xg[1][:], xw[1][:].indirect(offsets[:]))
+        cast_all("s", q1[1][0], raw11, 80, P)
+        cast_all("v", q1[1][0], raw11, 0, 80)
         quant_all(*q1[1])
-        for c in range(CHUNKS):
-            nc.vector.tensor_copy(
-                xg[1][:, c * CHUNK : (c + 1) * CHUNK],
-                xw[1][:].indirect(offsets[:, c * CHUNK // 16 : (c + 1) * CHUNK // 16]),
-            )
 
         def first_product(acc, qw, c):
             cols = slice(c * CHUNK, (c + 1) * CHUNK)
@@ -165,8 +161,8 @@ def tile_picked_modres_glusilu_p_kernel(
                         stop=(z == PASSES - 1),
                     )
 
-        cast_all("s", q3[0][0], raw30, 72, P)
-        cast_all("v", q3[0][0], raw30, 0, 72)
+        cast_all("s", q3[0][0], raw30, 80, P)
+        cast_all("v", q3[0][0], raw30, 0, 80)
         quant_all(*q3[0])
         cast("s", q3[1][0], raw31a, 0, 0, 64, 2)
         cast("v", q3[1][0], raw31a, 0, 0, 64, 0)

@@ -1,7 +1,6 @@
 from contextlib import ExitStack
 
 import concourse.mybir as mybir
-from concourse.masks import make_identity
 
 K, T, S, H, N = 1024, 1024, 512, 512, 256
 FLOPS = 2 * S * (2 * K * H + H * N)
@@ -42,13 +41,9 @@ def tile_picked_modres_glusilu_p_kernel(
         offsets = keep.tile([P, S // 16], U16, name="offsets")
         xs_win = sb("xs_win", [P, T], U8)
         w2_plane = sb("w2_plane", [P, N], U8)
-        gate_rows = sb("gate_rows", [P, P], F32)
-        ident = sb("ident", [P, P], F32)
 
         nc.gpsimd.memset(xs_win[:].bitcast(I32), 0)
         nc.gpsimd.memset(w2_plane[:].bitcast(I32), 0)
-        nc.gpsimd.memset(gate_rows[:], 0.0)
-        make_identity(nc, ident[:])
         warm = sb("warm", [P, 16], F32)
         nc.gpsimd.memset(warm[:], 0.0)
         nc.scalar.activation(out=warm[:, 8:9], in_=warm[:, 0:1], func=SILU)
@@ -79,27 +74,23 @@ def tile_picked_modres_glusilu_p_kernel(
         raw10 = load_w("raw10", w1, 0, 0, H)
         xw.append(load_x(1))
         raw11 = load_w("raw11", w1, 1, 0, H)
-        nc.sync.dma_start(out=gate_rows[0:CHUNKS, :], in_=gate[0:1, :].rearrange("o (c j) -> (o c) j", j=CHUNK))
-        raw30 = load_w("raw30", w3, 0, 0, H)
-        raw31a = load_w("raw31a", w3, 1, 0, H // 2)
-        raw31b = load_w("raw31b", w3, 1, H // 2, H)
-        res_src = [load_res("res_src%d" % b, b) for b in range(BLOCKS)]
-        w2_codes = sb("w2_codes", [P, 2 * N], U8)
-        nc.sync.dma_start(out=w2_codes[:].bitcast(I32), in_=w2_words[0].bitcast(I32))
         for q in range(4):
             nc.sync.dma_start(
                 out=w2_plane[32 * q : 32 * q + 4, :].bitcast(I32),
                 in_=w2_scales[0, 4 * q : 4 * q + 4, :].bitcast(I32),
             )
-        res_dst = [load_res("res_dst%d" % b, b) for b in range(BLOCKS)]
+        raw30 = load_w("raw30", w3, 0, 0, H)
+        raw31a = load_w("raw31a", w3, 1, 0, H // 2)
+        raw31b = load_w("raw31b", w3, 1, H // 2, H)
+        rows = [load_res("rows0", 0)]
+        w2_codes = sb("w2_codes", [P, 2 * N], U8)
+        nc.sync.dma_start(out=w2_codes[:].bitcast(I32), in_=w2_words[0].bitcast(I32))
+        gates = sb("gates", [P, S], F32)
+        nc.sync.dma_start(out=gates[:], in_=gate)
+        rows.append(load_res("rows1", 1))
 
         def bank(i, name, shape):
             return psum.tile(shape, F32, name=name, tag="bank%d" % i)
-
-        gate_ps = bank(7, "gate_ps", [P, P])
-        nc.tensor.transpose(gate_ps[:], gate_rows[:], ident[:])
-        gate_col = sb("gate_col", [P, CHUNKS], F32)
-        nc.scalar.copy(out=gate_col[:], in_=gate_ps[:, 0:CHUNKS])
 
         def cast(engine, wb, raw, m_first, m0, m1, t0):
             src = raw[:].rearrange("p j (m t) -> p m j t", t=PACK)[:, m0 - m_first : m1 - m_first, :, t0 : t0 + 2]
@@ -186,66 +177,59 @@ def tile_picked_modres_glusilu_p_kernel(
             first_product(acc, q3, c)
             up.append(acc)
 
-        picked = {}
-        gated = [sb("gated%d" % h, [P, BLOCKS, HALF], F32) for h in range(2)]
-        hb_last = sb("hb_last", [P, 2, CHUNK, PACK], BF16)
-        hb = [sb("hb0", [P, CHUNK, PACK], BF16)[:], sb("hb1", [P, CHUNK, PACK], BF16)[:], hb_last[:, 0], hb_last[:, 1]]
+        hb = [sb("hb%d" % h, [P, 2, CHUNK, PACK], BF16) for h in range(2)]
 
         def half_list(h):
             return offsets[:, h * HALF // 16 : (h + 1) * HALF // 16]
 
-        def pick(b, dst, places):
-            nc.vector.tensor_copy(dst, res_src[b][:].indirect(places))
-
         def hidden(c):
-            nc.vector.tensor_tensor(out=hb[c], in0=up[c][:].rearrange("p t n -> p n t"), in1=act[c], op=MULT)
+            nc.vector.tensor_tensor(out=hb[c // 2][:, c % 2], in0=up[c][:].rearrange("p t n -> p n t"), in1=act[c], op=MULT)
 
-        def quant_h(name, values, width, tag=None):
-            codes = sb("h_codes" + name, [P, width], U32, tag=tag)
-            plane = sb("h_plane" + name, [P, width], U8)
-            nc.vector.quantize_mx(out=codes[:].bitcast(FP8X4), scales=plane[:], in_=values)
+        def quant_h(h):
+            codes = sb("h_codes%d" % h, [P, HALF], U32)
+            plane = sb("h_plane%d" % h, [P, HALF], U8)
+            nc.vector.quantize_mx(out=codes[:].bitcast(FP8X4), scales=plane[:], in_=hb[h][:].rearrange("p c n t -> p (c n t)"))
             return codes, plane
 
-        def second(c, codes, plane):
-            y_t = bank(c if c < 2 else CHUNKS + c - 2, "y_t%d" % c, [P, N])
+        def second(b, h, codes, plane):
+            y = bank(2 * h + b, "y%d%d" % (b, h), [P, HALF])
             nc.tensor.matmul_mx(
-                out=y_t[:], lhsT=codes.bitcast(FP8X4), lhsT_scale=plane,
-                rhs=w2_codes[:].bitcast(FP4X4), rhs_scale=w2_plane[:], start=True, stop=True,
+                out=y[:], lhsT=w2_codes[:, 2 * b * P : 2 * (b + 1) * P].bitcast(FP4X4), lhsT_scale=w2_plane[:, b * P : (b + 1) * P],
+                rhs=codes[:].bitcast(FP8X4), rhs_scale=plane[:], start=True, stop=True,
             )
-            g_t = sb("g_t%d" % c, [P, N], F32)
-            nc.scalar.activation(out=g_t[:], in_=y_t[:], func=COPY, scale=gate_col[:, c : c + 1])
-            y_n = bank(CHUNKS + c, "y_n%d" % c, [P, BLOCKS, CHUNK])
-            for b in range(BLOCKS):
-                nc.tensor.transpose(y_n[:, b, :], g_t[:, b * P : (b + 1) * P], ident[:])
-            h, j0 = divmod(c * CHUNK, HALF)
-            nc.scalar.copy(out=gated[h][:, :, j0 : j0 + CHUNK], in_=y_n[:])
+            return y
 
-        def put(b, h):
-            nc.vector.tensor_tensor(res_dst[b][:].indirect(half_list(h)), gated[h][:, b, :], picked[b, h], ADD)
+        def gate_out(b, h, y):
+            g = sb("gated%d%d" % (b, h), [P, HALF], F32)
+            nc.vector.tensor_tensor(out=g[:], in0=y[:], in1=gates[:, h * HALF : (h + 1) * HALF], op=MULT)
+            return g
 
-        picked[0, 0] = late[:, PACK * S :]
-        pick(0, picked[0, 0], half_list(0))
+        old00 = late[:, PACK * S :]
+        nc.vector.tensor_copy(old00, rows[0][:].indirect(half_list(0)))
+        old01 = sb("old01", [P, HALF], F32, tag="w1_0_codes")
+        nc.scalar.activation(old01[:], rows[0][:].indirect(half_list(1)), COPY)
+        old1 = sb("old1", [P, S], F32, tag="w1_1_codes")
+        nc.scalar.activation(old1[:], rows[1][:].indirect(offsets[:]), COPY)
+        old0 = [old00, old01[:]]
+
         hidden(0)
         hidden(1)
-        up_last = sb("up_last", [P, CHUNK, PACK], F32)
-        nc.scalar.copy(out=up_last[:], in_=up[3][:].rearrange("p t n -> p n t"))
-        nc.gpsimd.tensor_tensor(out=hb[3], in0=up_last[:], in1=act[3], op=MULT)
-        for c in range(2):
-            codes, plane = quant_h(str(c), hb[c].rearrange("p n t -> p (n t)"), CHUNK)
-            second(c, codes[:], plane[:])
-        block1 = sb("picked1", [P, S], F32, tag="h_codes0")
-        pick(1, block1[:], offsets[:])
-        picked[1, 0], picked[1, 1] = block1[:, 0:HALF], block1[:, HALF:S]
+        made = [quant_h(0)]
         hidden(2)
-        picked[0, 1] = sb("picked01", [P, HALF], F32, tag="h_codes1")[:]
-        pick(0, picked[0, 1], half_list(1))
-        codes, plane = quant_h("23", hb_last[:].rearrange("p c n t -> p (c n t)"), 2 * CHUNK, tag="res_src1")
-        for c in (2, 3):
-            cols = slice((c - 2) * CHUNK, (c - 1) * CHUNK)
-            second(c, codes[:, cols], plane[:, cols])
-        put(0, 0)
-        put(1, 0)
-        put(0, 1)
-        nc.sync.dma_start(out=out[0:P, :], in_=res_dst[0][:])
-        put(1, 1)
-        nc.sync.dma_start(out=out[P : 2 * P, :], in_=res_dst[1][:])
+        y0 = [second(b, 0, *made[0]) for b in range(BLOCKS)]
+        g00 = gate_out(0, 0, y0[0])
+        hidden(3)
+        new0 = [sb("new0%d" % h, [P, HALF], F32) for h in range(2)]
+        nc.vector.tensor_tensor(out=new0[0][:], in0=g00[:], in1=old0[0], op=ADD)
+        nc.scalar.activation(rows[0][:].indirect(half_list(0)), new0[0][:], COPY)
+        made.append(quant_h(1))
+        g10 = gate_out(1, 0, y0[1])
+        y1 = [second(b, 1, *made[1]) for b in range(BLOCKS)]
+        g01 = gate_out(0, 1, y1[0])
+        g11 = gate_out(1, 1, y1[1])
+        nc.vector.tensor_tensor(out=new0[1][:], in0=g01[:], in1=old0[1], op=ADD)
+        nc.scalar.activation(rows[0][:].indirect(half_list(1)), new0[1][:], COPY)
+        nc.sync.dma_start(out=out[0:P, :], in_=rows[0][:])
+        nc.vector.tensor_tensor(rows[1][:].indirect(half_list(0)), g10[:], old1[:, 0:HALF], ADD)
+        nc.vector.tensor_tensor(rows[1][:].indirect(half_list(1)), g11[:], old1[:, HALF:S], ADD)
+        nc.sync.dma_start(out=out[P : 2 * P, :], in_=rows[1][:])

@@ -138,44 +138,48 @@ def tile_picked_modres_glusilu_p_kernel(
         cast_all("v", q1[1][0], raw11, 0, 80)
         quant_all(*q1[1])
 
-        def first_product(acc, qw, c):
+        def passes(acc, qw, c, z, order):
             cols = slice(c * CHUNK, (c + 1) * CHUNK)
-            for t in range(PACK):
-                for z in range(PASSES):
-                    nc.tensor.matmul_mx(
-                        out=acc[:, t, :],
-                        lhsT=qw[z][1][:, t * P : (t + 1) * P].bitcast(FP8X4),
-                        lhsT_scale=qw[z][2][:, t * P : (t + 1) * P],
-                        rhs=xg[z][:, cols].bitcast(FP8X4),
-                        rhs_scale=xs_g[4 * z : P, cols],
-                        start=(z == 0),
-                        stop=(z == PASSES - 1),
-                    )
+            for i, t in enumerate(order):
+                nc.tensor.matmul_mx(
+                    out=acc[:, t, :],
+                    lhsT=qw[z][1][:, t * P : (t + 1) * P].bitcast(FP8X4),
+                    lhsT_scale=qw[z][2][:, t * P : (t + 1) * P],
+                    rhs=xg[z][:, cols].bitcast(FP8X4),
+                    rhs_scale=xs_g[4 * z : P, cols],
+                    start=(z == 0 and i == 0),
+                    stop=(z == PASSES - 1 and i == PACK - 1),
+                )
 
         cast_all("s", q3[0][0], raw30, 80, P)
         cast_all("v", q3[0][0], raw30, 0, 80)
         quant_all(*q3[0])
         cast("s", q3[1][0], raw31a, 0, 0, 64, 2)
         cast("v", q3[1][0], raw31a, 0, 0, 64, 0)
+        for t in range(PACK):
+            quant(*q3[1], t, 0, 64)
         cast("s", q3[1][0], raw31b, 64, 64, P, 2)
         cast("v", q3[1][0], raw31b, 64, 64, P, 0)
         for t in range(PACK):
-            quant(*q3[1], t, 0, P)
+            quant(*q3[1], t, 64, P)
+
+        forward = list(range(PACK))
+        acc1 = [bank(c, "acc1_%d" % c, [P, PACK, CHUNK]) for c in range(CHUNKS)]
+        up = [bank(CHUNKS + c, "acc3_%d" % c, [P, PACK, CHUNK]) for c in range(CHUNKS)]
+        for z in range(PASSES):
+            for c in range(CHUNKS):
+                passes(acc1[c], q1, c, z, forward)
+        for c in range(CHUNKS):
+            passes(up[c], q3, c, 0, forward)
+        for c in range(CHUNKS):
+            passes(up[c], q3, c, 1, forward if c == 0 else forward[::-1])
 
         act = []
         late = sb("late", [P, PACK * S + HALF], F32, tag="raw31b")
         for c in range(CHUNKS):
-            acc = bank(c, "acc1_%d" % c, [P, PACK, CHUNK])
-            first_product(acc, q1, c)
             a = late[:, c * CHUNK * PACK : (c + 1) * CHUNK * PACK].rearrange("p (n t) -> p n t", t=PACK)
-            nc.scalar.activation(out=a, in_=acc[:].rearrange("p t n -> p n t"), func=SILU)
+            nc.scalar.activation(out=a, in_=acc1[c][:].rearrange("p t n -> p n t"), func=SILU)
             act.append(a)
-
-        up = []
-        for c in range(CHUNKS):
-            acc = bank(CHUNKS + c, "acc3_%d" % c, [P, PACK, CHUNK])
-            first_product(acc, q3, c)
-            up.append(acc)
 
         hb = [sb("hb%d" % h, [P, 2, CHUNK, PACK], BF16) for h in range(2)]
 

@@ -156,14 +156,17 @@ def tile_picked_modres_glusilu_p_kernel(
         quant_all(*q3[0])
         cast("s", q3[1][0], raw31a, 0, 0, 64, 2)
         cast("v", q3[1][0], raw31a, 0, 0, 64, 0)
-        for t in range(PACK):
+        for t in (2, 3):
             quant(*q3[1], t, 0, 64)
         cast("s", q3[1][0], raw31b, 64, 64, P, 2)
         cast("v", q3[1][0], raw31b, 64, 64, P, 0)
-        for t in range(PACK):
+        for t in (2, 3):
             quant(*q3[1], t, 64, P)
+        for t in (0, 1):
+            quant(*q3[1], t, 0, P)
 
         forward = list(range(PACK))
+        made = [2, 3, 0, 1]
         acc1 = [bank(c, "acc1_%d" % c, [P, PACK, CHUNK]) for c in range(CHUNKS)]
         up = [bank(CHUNKS + c, "acc3_%d" % c, [P, PACK, CHUNK]) for c in range(CHUNKS)]
         for z in range(PASSES):
@@ -172,7 +175,7 @@ def tile_picked_modres_glusilu_p_kernel(
         for c in range(CHUNKS):
             passes(up[c], q3, c, 0, forward)
         for c in range(CHUNKS):
-            passes(up[c], q3, c, 1, forward if c == 0 else forward[::-1])
+            passes(up[c], q3, c, 1, made if c == 0 else made[::-1])
 
         act = []
         late = sb("late", [P, PACK * S + HALF], F32, tag="raw31b")
@@ -186,8 +189,10 @@ def tile_picked_modres_glusilu_p_kernel(
         def half_list(h):
             return offsets[:, h * HALF // 16 : (h + 1) * HALF // 16]
 
-        def hidden(c):
-            nc.vector.tensor_tensor(out=hb[c // 2][:, c % 2], in0=up[c][:].rearrange("p t n -> p n t"), in1=act[c], op=MULT)
+        def hidden(c, n0=0, n1=CHUNK):
+            nc.vector.tensor_tensor(
+                out=hb[c // 2][:, c % 2, n0:n1], in0=up[c][:].rearrange("p t n -> p n t")[:, n0:n1], in1=act[c][:, n0:n1], op=MULT
+            )
 
         def quant_h(h):
             codes = sb("h_codes%d" % h, [P, HALF], U32)
@@ -203,9 +208,11 @@ def tile_picked_modres_glusilu_p_kernel(
             )
             return y
 
+        gated = [sb("gated%d" % b, [P, S], F32) for b in range(BLOCKS)]
+
         def gate_out(b, h, y):
-            g = sb("gated%d%d" % (b, h), [P, HALF], F32)
-            nc.vector.tensor_tensor(out=g[:], in0=y[:], in1=gates[:, h * HALF : (h + 1) * HALF], op=MULT)
+            g = gated[b][:, h * HALF : (h + 1) * HALF]
+            nc.vector.tensor_tensor(out=g, in0=y[:], in1=gates[:, h * HALF : (h + 1) * HALF], op=MULT)
             return g
 
         old00 = late[:, PACK * S :]
@@ -216,24 +223,25 @@ def tile_picked_modres_glusilu_p_kernel(
         nc.scalar.activation(old1[:], rows[1][:].indirect(offsets[:]), COPY)
         old0 = [old00, old01[:]]
 
+        new0 = [sb("new0%d" % h, [P, HALF], F32) for h in range(2)]
         hidden(0)
         hidden(1)
-        made = [quant_h(0)]
-        hidden(2)
-        y0 = [second(b, 0, *made[0]) for b in range(BLOCKS)]
+        hidden(2, 0, CHUNK // 2)
+        codes = [quant_h(0)]
+        y0 = [second(b, 0, *codes[0]) for b in range(BLOCKS)]
+        hidden(2, CHUNK // 2, CHUNK)
+        hidden(3, 0, CHUNK // 2)
         g00 = gate_out(0, 0, y0[0])
-        hidden(3)
-        new0 = [sb("new0%d" % h, [P, HALF], F32) for h in range(2)]
-        nc.vector.tensor_tensor(out=new0[0][:], in0=g00[:], in1=old0[0], op=ADD)
+        hidden(3, CHUNK // 2, CHUNK)
+        nc.vector.tensor_tensor(out=new0[0][:], in0=g00, in1=old0[0], op=ADD)
         nc.scalar.activation(rows[0][:].indirect(half_list(0)), new0[0][:], COPY)
-        made.append(quant_h(1))
-        g10 = gate_out(1, 0, y0[1])
-        y1 = [second(b, 1, *made[1]) for b in range(BLOCKS)]
+        codes.append(quant_h(1))
+        gate_out(1, 0, y0[1])
+        y1 = [second(b, 1, *codes[1]) for b in range(BLOCKS)]
         g01 = gate_out(0, 1, y1[0])
-        g11 = gate_out(1, 1, y1[1])
-        nc.vector.tensor_tensor(out=new0[1][:], in0=g01[:], in1=old0[1], op=ADD)
+        gate_out(1, 1, y1[1])
+        nc.vector.tensor_tensor(out=new0[1][:], in0=g01, in1=old0[1], op=ADD)
         nc.scalar.activation(rows[0][:].indirect(half_list(1)), new0[1][:], COPY)
         nc.sync.dma_start(out=out[0:P, :], in_=rows[0][:])
-        nc.vector.tensor_tensor(rows[1][:].indirect(half_list(0)), g10[:], old1[:, 0:HALF], ADD)
-        nc.vector.tensor_tensor(rows[1][:].indirect(half_list(1)), g11[:], old1[:, HALF:S], ADD)
+        nc.vector.tensor_tensor(rows[1][:].indirect(offsets[:]), gated[1][:], old1[:], ADD)
         nc.sync.dma_start(out=out[P : 2 * P, :], in_=rows[1][:])

@@ -156,17 +156,14 @@ def tile_picked_modres_glusilu_p_kernel(
         quant_all(*q3[0])
         cast("s", q3[1][0], raw31a, 0, 0, 64, 2)
         cast("v", q3[1][0], raw31a, 0, 0, 64, 0)
-        for t in (2, 3):
+        for t in range(PACK):
             quant(*q3[1], t, 0, 64)
         cast("s", q3[1][0], raw31b, 64, 64, P, 2)
         cast("v", q3[1][0], raw31b, 64, 64, P, 0)
-        for t in (2, 3):
+        for t in range(PACK):
             quant(*q3[1], t, 64, P)
-        for t in (0, 1):
-            quant(*q3[1], t, 0, P)
 
         forward = list(range(PACK))
-        made = [2, 3, 0, 1]
         acc1 = [bank(c, "acc1_%d" % c, [P, PACK, CHUNK]) for c in range(CHUNKS)]
         up = [bank(CHUNKS + c, "acc3_%d" % c, [P, PACK, CHUNK]) for c in range(CHUNKS)]
         for z in range(PASSES):
@@ -175,7 +172,7 @@ def tile_picked_modres_glusilu_p_kernel(
         for c in range(CHUNKS):
             passes(up[c], q3, c, 0, forward)
         for c in range(CHUNKS):
-            passes(up[c], q3, c, 1, made if c == 0 else made[::-1])
+            passes(up[c], q3, c, 1, forward if c == 0 else forward[::-1])
 
         act = []
         late = sb("late", [P, PACK * S + HALF], F32, tag="raw31b")

@@ -158,8 +158,9 @@ def tile_picked_modres_glusilu_p_kernel(
         cast("v", q3[1][0], raw31a, 0, 0, 64, 0)
         for t in range(PACK):
             quant(*q3[1], t, 0, 64)
-        cast("s", q3[1][0], raw31b, 64, 64, P, 2)
+        cast("s", q3[1][0], raw31b, 64, 64, 112, 2)
         cast("v", q3[1][0], raw31b, 64, 64, P, 0)
+        cast("v", q3[1][0], raw31b, 64, 112, P, 2)
         for t in range(PACK):
             quant(*q3[1], t, 64, P)
 
@@ -181,7 +182,9 @@ def tile_picked_modres_glusilu_p_kernel(
             nc.scalar.activation(out=a, in_=acc1[c][:].rearrange("p t n -> p n t"), func=SILU)
             act.append(a)
 
-        hb = [sb("hb%d" % h, [P, 2, CHUNK, PACK], BF16) for h in range(2)]
+        shared = sb("shared", [P, S - CHUNK + S], F32)
+        hb = [sb("hb0", [P, 2, CHUNK, PACK], BF16)[:]]
+        hb.append(shared[:, S - CHUNK :].bitcast(BF16).rearrange("p (c n t) -> p c n t", c=2, t=PACK))
 
         def half_list(h):
             return offsets[:, h * HALF // 16 : (h + 1) * HALF // 16]
@@ -194,7 +197,7 @@ def tile_picked_modres_glusilu_p_kernel(
         def quant_h(h):
             codes = sb("h_codes%d" % h, [P, HALF], U32)
             plane = sb("h_plane%d" % h, [P, HALF], U8)
-            nc.vector.quantize_mx(out=codes[:].bitcast(FP8X4), scales=plane[:], in_=hb[h][:].rearrange("p c n t -> p (c n t)"))
+            nc.vector.quantize_mx(out=codes[:].bitcast(FP8X4), scales=plane[:], in_=hb[h].rearrange("p c n t -> p (c n t)"))
             return codes, plane
 
         def second(b, h, codes, plane):
@@ -216,8 +219,8 @@ def tile_picked_modres_glusilu_p_kernel(
         nc.vector.tensor_copy(old00, rows[0][:].indirect(half_list(0)))
         old01 = sb("old01", [P, HALF], F32, tag="w1_0_codes")
         nc.scalar.activation(old01[:], rows[0][:].indirect(half_list(1)), COPY)
-        old1 = sb("old1", [P, S], F32, tag="w1_1_codes")
-        nc.scalar.activation(old1[:], rows[1][:].indirect(offsets[:]), COPY)
+        old1 = shared[:, 0:S]
+        nc.scalar.activation(old1[:, 0 : S - CHUNK], rows[1][:].indirect(offsets[:, 0 : (S - CHUNK) // 16]), COPY)
         old0 = [old00, old01[:]]
 
         new0 = [sb("new0%d" % h, [P, HALF], F32) for h in range(2)]
@@ -234,11 +237,12 @@ def tile_picked_modres_glusilu_p_kernel(
         nc.scalar.activation(rows[0][:].indirect(half_list(0)), new0[0][:], COPY)
         codes.append(quant_h(1))
         gate_out(1, 0, y0[1])
+        nc.vector.tensor_copy(old1[:, S - CHUNK : S], rows[1][:].indirect(offsets[:, (S - CHUNK) // 16 : S // 16]))
         y1 = [second(b, 1, *codes[1]) for b in range(BLOCKS)]
         g01 = gate_out(0, 1, y1[0])
         gate_out(1, 1, y1[1])
         nc.vector.tensor_tensor(out=new0[1][:], in0=g01, in1=old0[1], op=ADD)
         nc.scalar.activation(rows[0][:].indirect(half_list(1)), new0[1][:], COPY)
         nc.sync.dma_start(out=out[0:P, :], in_=rows[0][:])
-        nc.vector.tensor_tensor(rows[1][:].indirect(offsets[:]), gated[1][:], old1[:], ADD)
+        nc.vector.tensor_tensor(rows[1][:].indirect(offsets[:]), gated[1][:], old1, ADD)
         nc.sync.dma_start(out=out[P : 2 * P, :], in_=rows[1][:])

@@ -42,10 +42,10 @@ def tile_picked_modres_glusilu_p_kernel(
         xs_win = sb("xs_win", [P, T], U8)
         w2_plane = sb("w2_plane", [P, N], U8)
 
-        nc.gpsimd.memset(xs_win[:].bitcast(I32), 0)
-        nc.gpsimd.memset(w2_plane[:].bitcast(I32), 0)
+        nc.vector.memset(xs_win[:].bitcast(I32), 0)
+        nc.vector.memset(w2_plane[:].bitcast(I32), 0)
         warm = sb("warm", [P, 16], F32)
-        nc.gpsimd.memset(warm[:], 0.0)
+        nc.vector.memset(warm[:], 0.0)
         nc.scalar.activation(out=warm[:, 8:9], in_=warm[:, 0:1], func=SILU)
 
         def load_w(name, w, z, c0, c1):
@@ -64,8 +64,8 @@ def tile_picked_modres_glusilu_p_kernel(
             nc.sync.dma_start(out=tile[:], in_=res[b * P : (b + 1) * P, :])
             return tile
 
-        nc.sync.dma_start(offsets[:], offs)
         xw = [load_x(0)]
+        nc.sync.dma_start(offsets[:], offs)
         for q in range(4):
             nc.sync.dma_start(
                 out=xs_win[32 * q : 32 * q + 4 * PASSES, :].bitcast(I32),

@@ -229,6 +229,12 @@ def tile_picked_modres_glusilu_p_kernel(
         hidden(2, 0, CHUNK // 2)
         codes = [quant_h(0)]
         y0 = [second(b, 0, *codes[0]) for b in range(BLOCKS)]
+        spare = bank(CHUNKS, "spare", [P, BLOCKS, HALF])
+        for b in range(BLOCKS):
+            nc.tensor.matmul_mx(
+                out=spare[:, b, :], lhsT=w2_codes[:, 2 * b * P : 2 * (b + 1) * P].bitcast(FP4X4), lhsT_scale=w2_plane[:, b * P : (b + 1) * P],
+                rhs=codes[0][0][:].bitcast(FP8X4), rhs_scale=codes[0][1][:], start=True, stop=True,
+            )
         hidden(2, CHUNK // 2, CHUNK)
         hidden(3, 0, CHUNK // 2)
         g00 = gate_out(0, 0, y0[0])

@@ -36,7 +36,7 @@ def tile_picked_modres_glusilu_p_kernel(
         psum = ctx.enter_context(tc.psum_pool(name="psum", bufs=1))
 
         def sb(name, shape, dtype, tag=None):
-            return keep.tile(shape, dtype, name=name, tag=tag or name, align_bytes=64)
+            return keep.tile(shape, dtype, name=name, tag=tag or name, align_bytes=256)
 
         offsets = keep.tile([P, S // 16], U16, name="offsets")
         xs_win = sb("xs_win", [P, T], U8)

@@ -80,8 +80,11 @@ def tile_picked_modres_glusilu_p_kernel(
                 in_=w2_scales[0, 4 * q : 4 * q + 4, :].bitcast(I32),
             )
         raw30 = load_w("raw30", w3, 0, 0, H)
-        raw31a = load_w("raw31a", w3, 1, 0, H // 2)
-        raw31b = load_w("raw31b", w3, 1, H // 2, H)
+        raw31 = sb("raw31", [P, PACK, H], F32)
+        last_rows = w3[P * PACK : 2 * P * PACK, :].rearrange("(p j) c -> p (j c)", j=PACK)
+        cut = PACK * H - H // 2
+        for e0, e1 in ((0, cut), (cut, PACK * H)):
+            nc.sync.dma_start(out=raw31[:].rearrange("p j c -> p (j c)")[:, e0:e1], in_=last_rows[:, e0:e1])
         rows = [load_res("rows0", 0)]
         w2_codes = sb("w2_codes", [P, 2 * N], U8)
         nc.sync.dma_start(out=w2_codes[:].bitcast(I32), in_=w2_words[0].bitcast(I32))
@@ -154,15 +157,12 @@ def tile_picked_modres_glusilu_p_kernel(
         cast_all("s", q3[0][0], raw30, 80, P)
         cast_all("v", q3[0][0], raw30, 0, 80)
         quant_all(*q3[0])
-        cast("s", q3[1][0], raw31a, 0, 0, 64, 2)
-        cast("v", q3[1][0], raw31a, 0, 0, 64, 0)
+        for m0 in (0, 64):
+            cast("s", q3[1][0], raw31, 0, m0, m0 + 48, 2)
+            cast("v", q3[1][0], raw31, 0, m0, m0 + 64, 0)
+            cast("v", q3[1][0], raw31, 0, m0 + 48, m0 + 64, 2)
         for t in range(PACK):
-            quant(*q3[1], t, 0, 64)
-        cast("s", q3[1][0], raw31b, 64, 64, 112, 2)
-        cast("v", q3[1][0], raw31b, 64, 64, P, 0)
-        cast("v", q3[1][0], raw31b, 64, 112, P, 2)
-        for t in range(PACK):
-            quant(*q3[1], t, 64, P)
+            quant(*q3[1], t, 0, P)
 
         forward = list(range(PACK))
         acc1 = [bank(c, "acc1_%d" % c, [P, PACK, CHUNK]) for c in range(CHUNKS)]
@@ -176,7 +176,7 @@ def tile_picked_modres_glusilu_p_kernel(
             passes(up[c], q3, c, 1, forward if c == 0 else forward[::-1])
 
         act = []
-        late = sb("late", [P, PACK * S + HALF], F32, tag="raw31b")
+        late = sb("late", [P, PACK * S + HALF], F32, tag="raw31")
         for c in range(CHUNKS):
             a = late[:, c * CHUNK * PACK : (c + 1) * CHUNK * PACK].rearrange("p (n t) -> p n t", t=PACK)
             nc.scalar.activation(out=a, in_=acc1[c][:].rearrange("p t n -> p n t"), func=SILU)

@@ -25,6 +25,7 @@ CHUNK = 128
 CHUNKS = S // CHUNK
 HALF = S // 2
 BLOCKS = N // P
+RUN = 4
 
 
 def tile_picked_modres_glusilu_p_kernel(
@@ -178,8 +179,8 @@ def tile_picked_modres_glusilu_p_kernel(
         act = []
         late = sb("late", [P, PACK * S + HALF], F32, tag="raw31")
         for c in range(CHUNKS):
-            a = late[:, c * CHUNK * PACK : (c + 1) * CHUNK * PACK].rearrange("p (n t) -> p n t", t=PACK)
-            nc.scalar.activation(out=a, in_=acc1[c][:].rearrange("p t n -> p n t"), func=SILU)
+            a = late[:, c * CHUNK * PACK : (c + 1) * CHUNK * PACK].rearrange("p (g t n) -> p g t n", t=PACK, n=RUN)
+            nc.scalar.activation(out=a, in_=acc1[c][:].rearrange("p t (g n) -> p g t n", n=RUN), func=SILU)
             act.append(a)
 
         shared = sb("shared", [P, S - CHUNK + S], F32)
@@ -191,7 +192,10 @@ def tile_picked_modres_glusilu_p_kernel(
 
         def hidden(c, n0=0, n1=CHUNK):
             nc.vector.tensor_tensor(
-                out=hb[c // 2][:, c % 2, n0:n1], in0=up[c][:].rearrange("p t n -> p n t")[:, n0:n1], in1=act[c][:, n0:n1], op=MULT
+                out=hb[c // 2][:, c % 2].rearrange("p (g n) t -> p g t n", n=RUN)[:, n0 // RUN : n1 // RUN],
+                in0=up[c][:].rearrange("p t (g n) -> p g t n", n=RUN)[:, n0 // RUN : n1 // RUN],
+                in1=act[c][:, n0 // RUN : n1 // RUN],
+                op=MULT,
             )
 
         def quant_h(h):

@@ -233,10 +233,11 @@ def tile_picked_modres_glusilu_p_kernel(
         hidden(2, 0, CHUNK // 2)
         codes = [quant_h(0)]
         y0 = [second(b, 0, *codes[0]) for b in range(BLOCKS)]
-        spare = bank(CHUNKS, "spare", [P, BLOCKS, HALF])
-        for b in range(BLOCKS):
+        spare = [bank(CHUNKS + i, "spare%d" % i, [P, BLOCKS, HALF]) for i in range(2)]
+        for i in range(3):
+            b = i % BLOCKS
             nc.tensor.matmul_mx(
-                out=spare[:, b, :], lhsT=w2_codes[:, 2 * b * P : 2 * (b + 1) * P].bitcast(FP4X4), lhsT_scale=w2_plane[:, b * P : (b + 1) * P],
+                out=spare[i // BLOCKS][:, b, :], lhsT=w2_codes[:, 2 * b * P : 2 * (b + 1) * P].bitcast(FP4X4), lhsT_scale=w2_plane[:, b * P : (b + 1) * P],
                 rhs=codes[0][0][:].bitcast(FP8X4), rhs_scale=codes[0][1][:], start=True, stop=True,
             )
         hidden(2, CHUNK // 2, CHUNK)

from contextlib import ExitStack

import concourse.mybir as mybir

K, T, S, H, N = 1024, 1024, 512, 512, 256
FLOPS = 2 * S * (2 * K * H + H * N)

F32 = mybir.dt.float32
BF16 = mybir.dt.bfloat16
I32 = mybir.dt.int32
U32 = mybir.dt.uint32
U16 = mybir.dt.uint16
U8 = mybir.dt.uint8
FP8X4 = mybir.dt.float8_e4m3fn_x4
FP4X4 = mybir.dt.float4_e2m1fn_x4
MULT = mybir.AluOpType.mult
ADD = mybir.AluOpType.add
SILU = mybir.ActivationFunctionType.Silu
COPY = mybir.ActivationFunctionType.Copy

P = 128
PACK = 4
PASSES = K // (P * PACK)
CHUNK = 128
CHUNKS = S // CHUNK
HALF = S // 2
BLOCKS = N // P
RUN = 4


def tile_picked_modres_glusilu_p_kernel(
    tc, x_words, x_scales, gate, res, w1, w3, w2_words, w2_scales, offs, out
):
    nc = tc.nc
    with ExitStack() as ctx:
        keep = ctx.enter_context(tc.tile_pool(name="keep", bufs=1))
        psum = ctx.enter_context(tc.psum_pool(name="psum", bufs=1))

        def sb(name, shape, dtype, tag=None):
            return keep.tile(shape, dtype, name=name, tag=tag or name, align_bytes=256)

        offsets = keep.tile([P, S // 16], U16, name="offsets")
        xs_win = sb("xs_win", [P, T], U8)
        w2_plane = sb("w2_plane", [P, N], U8)

        nc.vector.memset(xs_win[:].bitcast(I32), 0)
        nc.vector.memset(w2_plane[:].bitcast(I32), 0)
        warm = sb("warm", [P, 16], F32)
        nc.vector.memset(warm[:], 0.0)
        nc.scalar.activation(out=warm[:, 8:9], in_=warm[:, 0:1], func=SILU)

        def load_w(name, w, z, c0, c1):
            raw = sb(name, [P, PACK, c1 - c0], F32)
            rows = w[z * P * PACK : (z + 1) * P * PACK, c0:c1]
            nc.sync.dma_start(out=raw[:], in_=rows.rearrange("(p j) c -> p j c", j=PACK))
            return raw

        def load_x(z):
            win = sb("xw%d" % z, [P, T], U32)
            nc.sync.dma_start(out=win[:].bitcast(I32), in_=x_words[z].rearrange("p c r -> p (c r)").bitcast(I32))
            return win

        def load_res(name, b):
            tile = sb(name, [P, T], F32)
            nc.sync.dma_start(out=tile[:], in_=res[b * P : (b + 1) * P, :])
            return tile

        xw = [load_x(0)]
        nc.sync.dma_start(offsets[:], offs)
        for q in range(4):
            nc.sync.dma_start(
                out=xs_win[32 * q : 32 * q + 4 * PASSES, :].bitcast(I32),
                in_=x_scales[:, 4 * q : 4 * q + 4, :].bitcast(I32),
            )
        raw10 = load_w("raw10", w1, 0, 0, H)
        xw.append(load_x(1))
        raw11 = load_w("raw11", w1, 1, 0, H)
        for q in range(4):
            nc.sync.dma_start(
                out=w2_plane[32 * q : 32 * q + 4, :].bitcast(I32),
                in_=w2_scales[0, 4 * q : 4 * q + 4, :].bitcast(I32),
            )
        raw30 = load_w("raw30", w3, 0, 0, H)
        raw31 = sb("raw31", [P, PACK, H], F32)
        last_rows = w3[P * PACK : 2 * P * PACK, :].rearrange("(p j) c -> p (j c)", j=PACK)
        cut = PACK * H - H // 2
        for e0, e1 in ((0, cut), (cut, PACK * H)):
            nc.sync.dma_start(out=raw31[:].rearrange("p j c -> p (j c)")[:, e0:e1], in_=last_rows[:, e0:e1])
        rows = [load_res("rows0", 0)]
        w2_codes = sb("w2_codes", [P, 2 * N], U8)
        nc.sync.dma_start(out=w2_codes[:].bitcast(I32), in_=w2_words[0].bitcast(I32))
        gates = sb("gates", [P, S], F32)
        nc.sync.dma_start(out=gates[:], in_=gate)
        rows.append(load_res("rows1", 1))

        def bank(i, name, shape):
            return psum.tile(shape, F32, name=name, tag="bank%d" % i)

        def cast(engine, wb, raw, m_first, m0, m1, t0):
            src = raw[:].rearrange("p j (m t) -> p m j t", t=PACK)[:, m0 - m_first : m1 - m_first, :, t0 : t0 + 2]
            dst = wb[:].rearrange("p t m j -> p m j t")[:, m0:m1, :, t0 : t0 + 2]
            if engine == "v":
                nc.vector.tensor_copy(out=dst, in_=src)
            else:
                nc.scalar.copy(out=dst, in_=src)

        def cast_all(engine, wb, raw, m0, m1):
            src = raw[:].rearrange("p j (m t) -> p m j t", t=PACK)[:, m0:m1]
            dst = wb[:].rearrange("p t m j -> p m j t")[:, m0:m1]
            if engine == "v":
                nc.vector.tensor_copy(out=dst, in_=src)
            else:
                nc.scalar.copy(out=dst, in_=src)

        def quant(wb, codes, plane, t, m0, m1):
            cols = slice(t * P + m0, t * P + m1)
            nc.vector.quantize_mx(
                out=codes[:, cols].bitcast(FP8X4),
                scales=plane[:, cols],
                in_=wb[:, t, m0:m1, :].rearrange("p m j -> p (m j)"),
            )

        def quant_all(wb, codes, plane):
            nc.vector.quantize_mx(out=codes[:].bitcast(FP8X4), scales=plane[:], in_=wb[:].rearrange("p t m j -> p (t m j)"))

        def w_tiles(name):
            return (sb(name + "_bf", [P, PACK, P, PACK], BF16), sb(name + "_codes", [P, H], U32), sb(name + "_plane", [P, H], U8))

        q1 = [w_tiles("w1_%d" % z) for z in range(PASSES)]
        q3 = [w_tiles("w3_%d" % z) for z in range(PASSES)]

        xs_g = sb("xs_g", [P, S], U8)
        xg = [sb("xg%d" % z, [P, S], U32) for z in range(PASSES)]

        nc.vector.tensor_copy(xg[0][:], xw[0][:].indirect(offsets[:]))
        nc.vector.tensor_copy(xs_g[:], xs_win[:].indirect(offsets[:]))
        cast_all("s", q1[0][0], raw10, 80, P)
        cast_all("v", q1[0][0], raw10, 0, 80)
        quant_all(*q1[0])
        nc.vector.tensor_copy(xg[1][:], xw[1][:].indirect(offsets[:]))
        cast_all("s", q1[1][0], raw11, 80, P)
        cast_all("v", q1[1][0], raw11, 0, 80)
        quant_all(*q1[1])

        def passes(acc, qw, c, z, order):
            cols = slice(c * CHUNK, (c + 1) * CHUNK)
            for i, t in enumerate(order):
                nc.tensor.matmul_mx(
                    out=acc[:, t, :],
                    lhsT=qw[z][1][:, t * P : (t + 1) * P].bitcast(FP8X4),
                    lhsT_scale=qw[z][2][:, t * P : (t + 1) * P],
                    rhs=xg[z][:, cols].bitcast(FP8X4),
                    rhs_scale=xs_g[4 * z : P, cols],
                    start=(z == 0 and i == 0),
                    stop=(z == PASSES - 1 and i == PACK - 1),
                )

        cast_all("s", q3[0][0], raw30, 80, P)
        cast_all("v", q3[0][0], raw30, 0, 80)
        quant_all(*q3[0])
        for m0 in (0, 64):
            cast("s", q3[1][0], raw31, 0, m0, m0 + 48, 2)
            cast("v", q3[1][0], raw31, 0, m0, m0 + 64, 0)
            cast("v", q3[1][0], raw31, 0, m0 + 48, m0 + 64, 2)
        for t in range(PACK):
            quant(*q3[1], t, 0, P)

        forward = list(range(PACK))
        acc1 = [bank(c, "acc1_%d" % c, [P, PACK, CHUNK]) for c in range(CHUNKS)]
        up = [bank(CHUNKS + c, "acc3_%d" % c, [P, PACK, CHUNK]) for c in range(CHUNKS)]
        for z in range(PASSES):
            for c in range(CHUNKS):
                passes(acc1[c], q1, c, z, forward)
        for c in range(CHUNKS):
            passes(up[c], q3, c, 0, forward)
        for c in range(CHUNKS):
            passes(up[c], q3, c, 1, forward if c == 0 else forward[::-1])

        act = []
        late = sb("late", [P, PACK * S + HALF], F32, tag="raw31")
        for c in range(CHUNKS):
            a = late[:, c * CHUNK * PACK : (c + 1) * CHUNK * PACK].rearrange("p (g t n) -> p g t n", t=PACK, n=RUN)
            nc.scalar.activation(out=a, in_=acc1[c][:].rearrange("p t (g n) -> p g t n", n=RUN), func=SILU)
            act.append(a)

        shared = sb("shared", [P, S - CHUNK + S], F32)
        hb = [sb("hb0", [P, 2, CHUNK, PACK], BF16)[:]]
        hb.append(shared[:, S - CHUNK :].bitcast(BF16).rearrange("p (c n t) -> p c n t", c=2, t=PACK))

        def half_list(h):
            return offsets[:, h * HALF // 16 : (h + 1) * HALF // 16]

        def hidden(c, n0=0, n1=CHUNK):
            nc.vector.tensor_tensor(
                out=hb[c // 2][:, c % 2].rearrange("p (g n) t -> p g t n", n=RUN)[:, n0 // RUN : n1 // RUN],
                in0=up[c][:].rearrange("p t (g n) -> p g t n", n=RUN)[:, n0 // RUN : n1 // RUN],
                in1=act[c][:, n0 // RUN : n1 // RUN],
                op=MULT,
            )

        def quant_h(h):
            codes = sb("h_codes%d" % h, [P, HALF], U32)
            plane = sb("h_plane%d" % h, [P, HALF], U8)
            nc.vector.quantize_mx(out=codes[:].bitcast(FP8X4), scales=plane[:], in_=hb[h].rearrange("p c n t -> p (c n t)"))
            return codes, plane

        def second(b, h, codes, plane):
            y = bank(2 * h + b, "y%d%d" % (b, h), [P, HALF])
            nc.tensor.matmul_mx(
                out=y[:], lhsT=w2_codes[:, 2 * b * P : 2 * (b + 1) * P].bitcast(FP4X4), lhsT_scale=w2_plane[:, b * P : (b + 1) * P],
                rhs=codes[:].bitcast(FP8X4), rhs_scale=plane[:], start=True, stop=True,
            )
            return y

        gated = [sb("gated%d" % b, [P, S], F32) for b in range(BLOCKS)]

        def gate_out(b, h, y):
            g = gated[b][:, h * HALF : (h + 1) * HALF]
            nc.vector.tensor_tensor(out=g, in0=y[:], in1=gates[:, h * HALF : (h + 1) * HALF], op=MULT)
            return g

        old00 = late[:, PACK * S :]
        nc.vector.tensor_copy(old00, rows[0][:].indirect(half_list(0)))
        old01 = sb("old01", [P, HALF], F32, tag="w1_0_codes")
        nc.scalar.activation(old01[:], rows[0][:].indirect(half_list(1)), COPY)
        old1 = shared[:, 0:S]
        nc.scalar.activation(old1[:, 0 : S - CHUNK], rows[1][:].indirect(offsets[:, 0 : (S - CHUNK) // 16]), COPY)
        old0 = [old00, old01[:]]

        new0 = [sb("new0%d" % h, [P, HALF], F32) for h in range(2)]
        hidden(0)
        hidden(1)
        hidden(2, 0, CHUNK // 2)
        codes = [quant_h(0)]
        y0 = [second(b, 0, *codes[0]) for b in range(BLOCKS)]
        spare = [bank(CHUNKS + i, "spare%d" % i, [P, BLOCKS, HALF]) for i in range(2)]
        for i in range(3):
            b = i % BLOCKS
            nc.tensor.matmul_mx(
                out=spare[i // BLOCKS][:, b, :], lhsT=w2_codes[:, 2 * b * P : 2 * (b + 1) * P].bitcast(FP4X4), lhsT_scale=w2_plane[:, b * P : (b + 1) * P],
                rhs=codes[0][0][:].bitcast(FP8X4), rhs_scale=codes[0][1][:], start=True, stop=True,
            )
        hidden(2, CHUNK // 2, CHUNK)
        hidden(3, 0, CHUNK // 2)
        g00 = gate_out(0, 0, y0[0])
        hidden(3, CHUNK // 2, CHUNK)
        nc.vector.tensor_tensor(out=new0[0][:], in0=g00, in1=old0[0], op=ADD)
        nc.scalar.activation(rows[0][:].indirect(half_list(0)), new0[0][:], COPY)
        codes.append(quant_h(1))
        gate_out(1, 0, y0[1])
        nc.vector.tensor_copy(old1[:, S - CHUNK : S], rows[1][:].indirect(offsets[:, (S - CHUNK) // 16 : S // 16]))
        y1 = [second(b, 1, *codes[1]) for b in range(BLOCKS)]
        g01 = gate_out(0, 1, y1[0])
        gate_out(1, 1, y1[1])
        nc.vector.tensor_tensor(out=new0[1][:], in0=g01, in1=old0[1], op=ADD)
        nc.scalar.activation(rows[0][:].indirect(half_list(1)), new0[1][:], COPY)
        nc.sync.dma_start(out=out[0:P, :], in_=rows[0][:])
        nc.vector.tensor_tensor(rows[1][:].indirect(offsets[:]), gated[1][:], old1, ADD)
        nc.sync.dma_start(out=out[P : 2 * P, :], in_=rows[1][:])
